import numpy as np
import ml_dtypes


def mxq(x, axis, fmt="e4m3"):
    dtype, down = {"e4m3": (ml_dtypes.float8_e4m3fn, 7), "e5m2": (ml_dtypes.float8_e5m2, 14)}[fmt]
    v = np.moveaxis(np.asarray(x, np.float32).astype(ml_dtypes.bfloat16).astype(np.float64), axis, -1)
    blocks = v.reshape(v.shape[:-1] + (-1, 32))
    amax = np.abs(blocks).max(-1, keepdims=True)
    byte = np.maximum(np.where(amax > 0, np.frexp(amax)[1] - 1 + 127, 0) - down, 1)
    scale = np.exp2(byte - 127.0)
    codes = (blocks / scale).astype(np.float32).astype(dtype).astype(np.float64)
    return np.moveaxis((codes * scale).reshape(v.shape), -1, axis)


WIDE = False


def mx_kscale(k):
    if not WIDE:
        return np.ones(k)
    levels = np.array([10, -10, 5, -5, 0])
    if k % 512:
        return np.exp2(np.random.permutation(np.resize(levels, k // 32))).repeat(32)
    a = np.empty((k // 512, 16))
    for p in range(k // 512):
        a[p, :8] = np.random.permutation(np.resize(levels, 8))
        for g in range(8):
            far = levels[np.abs(levels - a[p, g]) >= 10]
            a[p, g + 8] = far[np.random.randint(len(far))]
    return np.exp2(a.ravel()).repeat(32)


def f64(x):
    return np.asarray(x).astype(np.float64)


def striped(idx):
    return np.tile(idx.reshape(-1, 16).T, (8, 1)).astype(np.uint16)


def unstriped(offs):
    return offs[:16].T.reshape(-1).astype(np.int64)


E2M1 = np.array([0.0, 0.5, 1.0, 1.5, 2.0, 3.0, 4.0, 6.0, -0.0, -0.5, -1.0, -1.5, -2.0, -3.0, -4.0, -6.0])


def pack_weight(w, fmt):
    k, n = w.shape
    w = f64(np.asarray(w, np.float32).astype(ml_dtypes.bfloat16)).reshape(k // 32, 32, n)
    amax = np.abs(w).max(1)
    if fmt == "e4m3":
        byte = np.frexp(amax)[1] - 1 + 127 - 7
    else:
        mant, ex = np.frexp(amax / 6.0)
        byte = np.where(mant > 0.5, ex, ex - 1) + 127
    byte = np.clip(np.where(amax > 0, byte, 1), 1, 254)
    scaled = (w * np.exp2(127.0 - byte)[:, None, :]).reshape(k, n).astype(np.float32)
    by_word = np.ascontiguousarray(scaled.reshape(k // 512, 128, 4, n).transpose(0, 1, 3, 2))
    if fmt == "e4m3":
        words = by_word.astype(ml_dtypes.float8_e4m3fn).view(np.uint8)
    else:
        c = by_word.astype(ml_dtypes.float4_e2m1fn).view(np.uint8) & 0xF
        words = (c[..., 0::2] | (c[..., 1::2] << 4)).reshape(k // 512, 128, 2 * n)
    return np.ascontiguousarray(words), np.ascontiguousarray(byte.astype(np.uint8).reshape(k // 512, 16, n))


def unpack_weight(words, scales, fmt):
    g, _, n = scales.shape
    words = np.ascontiguousarray(words).reshape(g, 128, n, -1)
    if fmt == "e4m3":
        vals = words.view(ml_dtypes.float8_e4m3fn).astype(np.float64)
    else:
        nib = np.empty((g, 128, n, 4), np.uint8)
        nib[..., 0::2] = words & 0xF
        nib[..., 1::2] = words >> 4
        vals = E2M1[nib]
    vals = vals * np.repeat(np.exp2(scales.astype(np.float64) - 127.0), 8, axis=1)[..., None]
    return vals.transpose(0, 1, 3, 2).reshape(g * 512, n)


def gelu(v):
    return 0.5 * v * (1.0 + np.tanh(np.sqrt(2.0 / np.pi) * (v + 0.044715 * v**3)))


def bf(x):
    return np.asarray(x, np.float32).astype(ml_dtypes.bfloat16)


def planes(Y):
    n, m = Y.shape
    b = f64(bf(Y)).reshape(n // 32, 32, m)
    amax = np.abs(b).max(1)
    byte = np.clip(np.where(amax > 0, np.frexp(amax)[1] - 1 + 127 - 7, 1), 1, 254)
    codes = (b * np.exp2(127.0 - byte)[:, None, :]).reshape(n, m).astype(np.float32).astype(ml_dtypes.float8_e4m3fn).view(np.uint8)
    words = codes.reshape(n // 512, 128, 4, m).transpose(0, 1, 3, 2)
    return np.ascontiguousarray(words), np.ascontiguousarray(byte.astype(np.uint8).reshape(n // 512, 16, m))


K, T, S, H, T2, P, N = 1536, 2048, 512, 1024, 1024, 512, 768

def setup_inputs():
    n = np.random.standard_normal
    s = mx_kscale(K)[:, None]
    u = mx_kscale(H)[:, None]
    d = {}
    d["tab_words"], d["tab_scales"] = pack_weight(n((K, T)) * s, "e4m3")
    d["offs"] = striped(np.random.permutation(T)[:S])
    d["offs2"] = striped(np.random.permutation(T2)[:S])
    d["offs3"] = striped(np.random.permutation(T2)[:P])
    d["w1"] = (2.0 * n((K, H)) / s * u.T / K ** 0.5).astype(np.float32)
    d["w2_words"], d["w2_scales"] = pack_weight(1.5 * n((K, H)) / s / K ** 0.5, "e2m1")
    d["wgs"] = np.exp(0.3 * n((128, S))).astype(np.float32)
    d["page0"] = (n((H, T2)) * u).astype(np.float32)
    d["gin"] = (1.3 * np.exp(0.3 * n(H)) / u[:, 0]).astype(np.float32)
    d["gain"] = (np.exp(0.4 * n(H)) * u[:, 0]).astype(np.float32)
    d["w3"] = (1.3 * n((H, N)) / u / H ** 0.5).astype(np.float32)
    return d

def reference(tab_words, tab_scales, offs, offs2, offs3, w1, w2_words, w2_scales,
              wgs, page0, gin, gain, w3):
    v = unpack_weight(tab_words, tab_scales, "e4m3")[:, unstriped(offs)]
    w2 = unpack_weight(w2_words, w2_scales, "e2m1")
    a = mxq(f64(w1), 0, "e4m3").T @ v
    b = w2.T @ v
    h = a / (1.0 + np.abs(b))
    page = f64(page0).copy()
    page[:, unstriped(offs2)] = np.tile(f64(wgs), (H // 128, 1)) * h
    x = f64(gain)[:, None] * np.tanh(f64(gin)[:, None] * page[:, unstriped(offs3)])
    y = mxq(f64(w3), 0, "e4m3").T @ mxq(x, 0, "e4m3")
    words, scales = planes(page)
    return y, page, words, scales

@@ -1,0 +1,367 @@
+from contextlib import ExitStack
+
+import concourse.mybir as mybir
+
+K, T, S, H, T2, M, N = 1536, 2048, 512, 1024, 1024, 512, 768
+FLOPS = 2 * (2 * K * H * S + H * N * M)
+
+F32 = mybir.dt.float32
+BF16 = mybir.dt.bfloat16
+I32 = mybir.dt.int32
+U32 = mybir.dt.uint32
+U16 = mybir.dt.uint16
+U8 = mybir.dt.uint8
+FP8X4 = mybir.dt.float8_e4m3fn_x4
+FP4X4 = mybir.dt.float4_e2m1fn_x4
+ACT = mybir.ActivationFunctionType
+MULT = mybir.AluOpType.mult
+
+P = 128
+PACK = 4
+KP = P * PACK
+PASSES = K // KP
+GROUPS = H // KP
+QUADS = 4
+HALF = T2 // 2
+
+
+def tile_list_membrane_cleaning_features_kernel(
+    tc, tab_words, tab_scales, offs, offs2, offs3, w1, w2_words, w2_scales, wgs, page0, gin, gain, w3,
+    out_0, out_1, out_2, out_3,
+):
+    nc = tc.nc
+    with ExitStack() as ctx:
+        lists = ctx.enter_context(tc.tile_pool(name="lists", bufs=1))
+        first = ctx.enter_context(tc.tile_pool(name="first", bufs=1))
+        psum = ctx.enter_context(tc.psum_pool(name="psum", bufs=1))
+
+        def bank(i):
+            return psum.tile([P, 512], F32, name="bank%d" % i, tag="bank%d" % i)
+
+        def stage_tile():
+            return ring.tile([P, 2048], BF16, name="stage", tag="raw", bufs=4, align_bytes=64)
+
+        def held_tile(a, dtype, width):
+            return ring.tile([P, width], dtype, name="held", tag="held%d" % a, bufs=1, align_bytes=64)
+
+        def quantize(codes, scales, staged):
+            nc.vector.quantize_mx(out=codes.bitcast(FP8X4), scales=scales, in_=staged)
+
+        def interleave(copy, staged, rows):
+            copy(
+                staged.rearrange("p (c i t) -> p c t i", i=4, t=PACK),
+                rows.rearrange("p t (c i) -> p c t i", i=4),
+            )
+
+        tab_sc = first.tile([P, PASSES, T], U8, name="tab_sc", tag="bytes", bufs=2, align_bytes=64)
+        w2_sc_raw = first.tile([P, PASSES, H], U8, name="w2_sc_raw", align_bytes=64)
+        nc.vector.memset(tab_sc[:, 0:2, :].bitcast(I32), 0)
+        nc.gpsimd.memset(tab_sc[:, 2, :].bitcast(I32), 0)
+        with tc.tile_pool(name="zero", bufs=1) as zero_pool:
+            zeros = zero_pool.tile([P, H // 4], I32, name="zeros")
+            nc.vector.memset(zeros[:], 0)
+            for a in range(PASSES):
+                nc.vector.tensor_copy(w2_sc_raw[:, a, :].bitcast(I32), zeros[:])
+        keep = ctx.enter_context(tc.tile_pool(name="keep", bufs=1))
+        ring = keep
+
+        idx1 = lists.tile([P, S // 16], U16, name="idx1")
+        idx2 = lists.tile([P, S // 16], U16, name="idx2")
+        idx3 = lists.tile([P, M // 16], U16, name="idx3")
+        nc.sync.dma_start(idx1[:], offs)
+        nc.sync.dma_start(idx2[:], offs2)
+        nc.sync.dma_start(idx3[:], offs3)
+        w2_raw = first.tile([P, PASSES, 2 * H], U8, name="w2_raw", tag="bytes", bufs=2, align_bytes=64)
+        nc.sync.dma_start(w2_raw[:].bitcast(I32), w2_words.rearrange("a p c -> p a c").bitcast(I32))
+
+        def load_scale_rows(tile, dram, q):
+            nc.sync.dma_start(
+                tile[32 * q : 32 * q + 4, :, :].bitcast(I32),
+                dram[:, 4 * q : 4 * q + 4, :].rearrange("a r c -> r a c").bitcast(I32),
+            )
+
+        tab_w = []
+
+        def load_table(a):
+            words = ring.tile([P, T], U32, name="tab_w", tag="early", bufs=3, align_bytes=64)
+            nc.sync.dma_start(words[:].bitcast(I32), tab_words[a].rearrange("p t i -> p (t i)").bitcast(I32))
+            tab_w.append(words)
+
+        for q in range(QUADS):
+            load_scale_rows(tab_sc, tab_scales, q)
+        load_table(0)
+        for q in (0, 1):
+            load_scale_rows(w2_sc_raw, w2_scales, q)
+        load_table(1)
+        for q in (2, 3):
+            load_scale_rows(w2_sc_raw, w2_scales, q)
+        load_table(2)
+
+        w1_raw = {}
+
+        def load_w1(g, a):
+            if g == 0 and a < 2:
+                raw = ring.tile([P, PACK, KP], F32, name="w1_raw", tag="group%d" % a, bufs=1)
+            else:
+                raw = ring.tile([P, PACK, KP], F32, name="w1_raw", tag="raw", bufs=4, align_bytes=64)
+            nc.sync.dma_start(
+                raw[:], w1[KP * a : KP * (a + 1), KP * g : KP * (g + 1)].rearrange("(p j) c -> p j c", j=PACK)
+            )
+            w1_raw[g, a] = raw
+
+        def dealt_rows(dram, g, t):
+            return dram[KP * g : KP * (g + 1), :].rearrange("(p t) c -> t p c", t=PACK)[t]
+
+        def load_page(g, t):
+            tile = keep.tile([P, T2], F32, name="page%d%d" % (g, t))
+            nc.sync.dma_start(tile[:], dealt_rows(page0, g, t))
+            return tile
+
+        for a in range(PASSES):
+            load_w1(0, a)
+        wg = keep.tile([P, PACK, S], F32, name="wg")
+        for q in (0, 2, 1, 3):
+            nc.sync.dma_start(wg[32 * q : 32 * (q + 1), :, :], wgs.rearrange("(p t) j -> p t j", t=PACK))
+        page = {(0, 0): load_page(0, 0)}
+        for a in range(PASSES):
+            page[0, a + 1] = load_page(0, a + 1)
+            load_w1(1, a)
+        gin_t = keep.tile([P, GROUPS, PACK], F32, name="gin_t")
+        gain_t = keep.tile([P, GROUPS, PACK], F32, name="gain_t")
+        nc.sync.dma_start(gin_t[:], gin.rearrange("(g p t) -> p g t", g=GROUPS, t=PACK))
+        nc.sync.dma_start(gain_t[:], gain.rearrange("(g p t) -> p g t", g=GROUPS, t=PACK))
+        for t in range(PACK):
+            page[1, t] = load_page(1, t)
+        w3_raw = []
+
+        def load_w3():
+            for g in range(GROUPS):
+                raw = ring.tile([P, PACK, 512], F32, name="w3_raw", tag="early", bufs=3, align_bytes=64)
+                nc.sync.dma_start(raw[:], w3[KP * g : KP * (g + 1), 0:512].rearrange("(p j) c -> p j c", j=PACK))
+                w3_raw.append(raw)
+            rest = ring.tile([P, GROUPS, PACK, N - 512], F32, name="w3_rest", tag="early", bufs=3, align_bytes=64)
+            for g in range(GROUPS):
+                nc.sync.dma_start(
+                    rest[:, g, :, :], w3[KP * g : KP * (g + 1), 512:N].rearrange("(p j) c -> p j c", j=PACK)
+                )
+            w3_raw.append(rest)
+
+        w2_c = [keep.tile([P, PASSES, 2 * KP], U8, name="w2_c%d" % g, align_bytes=64) for g in range(GROUPS)]
+        w2_s = [keep.tile([P, PASSES, KP], U8, name="w2_s%d" % g, align_bytes=64) for g in range(GROUPS)]
+
+        def deal_w2_words(g):
+            nc.vector.tensor_copy(
+                w2_c[g][:].bitcast(U16).rearrange("p a (t m) -> p t a m", t=PACK),
+                w2_raw[:].bitcast(U16)[:, :, KP * g : KP * (g + 1)].rearrange("p a (m t) -> p t a m", t=PACK),
+            )
+
+        def deal_w2_scales(g):
+            nc.vector.tensor_copy(
+                w2_s[g][:].rearrange("p a (t m) -> p t a m", t=PACK),
+                w2_sc_raw[:, :, KP * g : KP * (g + 1)].rearrange("p a (m t) -> p t a m", t=PACK),
+            )
+
+        deal_w2_words(0)
+        v_w, v_planes = [], []
+        for a in range(PASSES):
+            plane = keep.tile([P, S], U8, name="v_s%d" % a, align_bytes=64)
+            nc.vector.tensor_copy(plane[:], tab_sc[:, a, :].indirect(idx1[:]))
+            v_planes.append(plane)
+        deal_w2_scales(0)
+        for a in range(PASSES):
+            picked = keep.tile([P, S], U32, name="v_w%d" % a, align_bytes=64)
+            nc.vector.tensor_copy(picked[:], tab_w[a][:].indirect(idx1[:]))
+            v_w.append(picked)
+
+        damp = {}
+
+        def damping(g, t):
+            acc = bank(4 + t)
+            for a in range(PASSES):
+                nc.tensor.matmul_mx(
+                    out=acc[:],
+                    lhsT=w2_c[g][:, a, 2 * P * t : 2 * P * (t + 1)].bitcast(FP4X4),
+                    lhsT_scale=w2_s[g][:, a, P * t : P * (t + 1)],
+                    rhs=v_w[a][:].bitcast(FP8X4),
+                    rhs_scale=v_planes[a][:],
+                    start=(a == 0),
+                    stop=(a == PASSES - 1),
+                )
+            if g == 0 and t > 0:
+                size = held_tile(t - 1, F32, S)
+            elif g == 0:
+                size = ring.tile([P, S], F32, name="size", tag="group0", bufs=1)
+            else:
+                size = ring.tile([P, S], F32, name="size", tag="act", bufs=2)
+            nc.scalar.activation(size[:], acc[:], ACT.Abs)
+            root = ring.tile([P, S], F32, name="root", tag="damp", bufs=8)
+            nc.scalar.activation(root[:], size[:], ACT.Abs_reciprocal_sqrt, bias=1.0)
+            nc.scalar.activation(root[:], root[:], ACT.Square)
+            damp[g, t] = root
+
+        w1_c, w1_s = {}, {}
+
+        def quantize_w1(g, a, copy):
+            staged = held_tile(a, BF16, 2048)
+            copy(
+                staged[:].rearrange("p (t m j) -> p m j t", t=PACK, j=PACK),
+                w1_raw[g, a][:].rearrange("p j (m t) -> p m j t", t=PACK),
+            )
+            w1_c[g, a] = keep.tile([P, KP], U32, name="w1_c%d%d" % (g, a), align_bytes=64)
+            w1_s[g, a] = keep.tile([P, KP], U8, name="w1_s%d%d" % (g, a), align_bytes=64)
+            quantize(w1_c[g, a][:], w1_s[g, a][:], staged[:])
+
+        def first_products(g, first_bank):
+            accs = [bank(first_bank + t) for t in range(PACK)]
+            for a in range(PASSES):
+                for t in range(PACK):
+                    nc.tensor.matmul_mx(
+                        out=accs[t][:],
+                        lhsT=w1_c[g, a][:, P * t : P * (t + 1)].bitcast(FP8X4),
+                        lhsT_scale=w1_s[g, a][:, P * t : P * (t + 1)],
+                        rhs=v_w[a][:].bitcast(FP8X4),
+                        rhs_scale=v_planes[a][:],
+                        start=(a == 0),
+                        stop=(a == PASSES - 1),
+                    )
+            return accs
+
+        x_rows = {}
+
+        def renew(g, t, acc):
+            weighted = ring.tile([P, S], F32, name="weighted", tag="weighted", bufs=3)
+            nc.vector.tensor_tensor(weighted[:], acc[:], wg[:, t, :], MULT)
+            nc.vector.tensor_tensor(page[g, t][:].indirect(idx2[:]), weighted[:], damp[g, t][:], MULT)
+
+        def features(g, t):
+            cells = ring.tile([P, M], F32, name="cells", tag="cells", bufs=4)
+            nc.vector.tensor_copy(cells[:], page[g, t][:].indirect(idx3[:]))
+            if g == 0:
+                bent = ring.tile([P, M], F32, name="bent", tag="act", bufs=2)
+            else:
+                bent = ring.tile([P, M], F32, name="bent", tag="early", bufs=3, align_bytes=64)
+            nc.scalar.activation(bent[:], cells[:], ACT.Tanh, scale=gin_t[:, g, t : t + 1])
+            if t == 0:
+                x_rows[g] = first.tile([P, PACK, M], BF16, name="x_rows", tag="bytes", bufs=2, align_bytes=64)
+            nc.scalar.activation(x_rows[g][:, t, :], bent[:], ACT.Copy, scale=gain_t[:, g, t : t + 1])
+
+        grouped = {}
+
+        def regroup(g, t):
+            for h in range(2):
+                if t == 0:
+                    grouped[g, h] = ring.tile([P, PACK, HALF], F32, name="grouped", tag="group%d" % h, bufs=1)
+                nc.sync.dma_start(grouped[g, h][:, t, :], page[g, t][:, HALF * h : HALF * (h + 1)])
+
+        def store_page(g):
+            for h in range(2):
+                rows = out_1[KP * g : KP * (g + 1), HALF * h : HALF * (h + 1)]
+                nc.sync.dma_start(rows.rearrange("(p t) c -> p t c", t=PACK), grouped[g, h][:])
+
+        page_c, page_s = {}, {}
+
+        def planes(g, copies):
+            page_c[g] = keep.tile([P, T2], U32, name="page_c%d" % g, align_bytes=64)
+            page_s[g] = keep.tile([P, T2], U8, name="page_s%d" % g, align_bytes=64)
+            for h in range(2):
+                cols = slice(HALF * h, HALF * (h + 1))
+                staged = stage_tile()
+                interleave(copies[h], staged[:], grouped[g, h][:])
+                quantize(page_c[g][:, cols], page_s[g][:, cols], staged[:])
+
+        def store_planes(g):
+            nc.sync.dma_start(out_2[g].rearrange("p m t -> p (m t)").bitcast(I32), page_c[g][:].bitcast(I32))
+            for q in range(QUADS):
+                nc.sync.dma_start(
+                    out_3[g, 4 * q : 4 * q + 4, :].bitcast(I32), page_s[g][32 * q : 32 * q + 4, :].bitcast(I32)
+                )
+
+        x_c, x_s = {}, {}
+
+        def quantize_x(g, copy):
+            staged = stage_tile()
+            interleave(copy, staged[:], x_rows[g][:])
+            x_c[g] = keep.tile([P, M], U32, name="x_c%d" % g, align_bytes=64)
+            x_s[g] = keep.tile([P, M], U8, name="x_s%d" % g, align_bytes=64)
+            quantize(x_c[g][:], x_s[g][:], staged[:])
+
+        w3_c, w3_s = {}, {}
+
+        def quantize_w3():
+            for g in range(GROUPS):
+                staged = held_tile(g, BF16, 2048)
+                interleave(nc.scalar.copy, staged[:], w3_raw[g][:])
+                codes = keep.tile([P, 512], U32, name="w3_c%d" % g, align_bytes=64)
+                scales = keep.tile([P, 512], U8, name="w3_s%d" % g, align_bytes=64)
+                quantize(codes[:], scales[:], staged[:])
+                for n in range(4):
+                    w3_c[g, n] = codes[:, P * n : P * (n + 1)]
+                    w3_s[g, n] = scales[:, P * n : P * (n + 1)]
+            staged = held_tile(2, BF16, 2048)
+            for g in range(GROUPS):
+                interleave(nc.scalar.copy, staged[:, 1024 * g : 1024 * (g + 1)], w3_raw[2][:, g, :, :])
+            codes = keep.tile([P, 512], U32, name="w3_c2", align_bytes=64)
+            scales = keep.tile([P, 512], U8, name="w3_s2", align_bytes=64)
+            quantize(codes[:], scales[:], staged[:])
+            for g in range(GROUPS):
+                for n in range(4, N // P):
+                    cols = slice(256 * g + P * (n - 4), 256 * g + P * (n - 3))
+                    w3_c[g, n] = codes[:, cols]
+                    w3_s[g, n] = scales[:, cols]
+
+        def last_pass(g, n, acc):
+            nc.tensor.matmul_mx(
+                out=acc[:],
+                lhsT=w3_c[g, n].bitcast(FP8X4),
+                lhsT_scale=w3_s[g, n],
+                rhs=x_c[g][:].bitcast(FP8X4),
+                rhs_scale=x_s[g][:],
+                start=(g == 0),
+                stop=(g == GROUPS - 1),
+            )
+
+        quantize_w1(0, 0, nc.scalar.copy)
+        damping(0, 0)
+        for a in range(1, PASSES):
+            quantize_w1(0, a, nc.vector.tensor_copy)
+        accs = first_products(0, 0)
+        for t in range(1, PACK):
+            damping(0, t)
+        deal_w2_words(1)
+        deal_w2_scales(1)
+        for t in range(PACK):
+            renew(0, t, accs[t])
+        for a in range(PASSES):
+            quantize_w1(1, a, nc.scalar.copy)
+        for t in range(PACK):
+            damping(1, t)
+        accs = first_products(1, 0)
+        for t in range(PACK):
+            features(0, t)
+            regroup(0, t)
+        load_w3()
+        store_page(0)
+        for t in range(PACK):
+            renew(1, t, accs[t])
+        planes(0, (nc.scalar.copy, nc.scalar.copy))
+        quantize_x(0, nc.scalar.copy)
+        quantize_w3()
+        for t in range(PACK):
+            features(1, t)
+            regroup(1, t)
+        store_page(1)
+        store_planes(0)
+        y_acc = [bank((n + 4) % 8) for n in range(N // P)]
+        for n in range(N // P):
+            last_pass(0, n, y_acc[n])
+        quantize_x(1, nc.vector.tensor_copy)
+        for n in range(N // P):
+            last_pass(1, n, y_acc[n])
+            result = ring.tile([P, M], F32, name="result", tag="damp", bufs=8)
+            if n % 2 == 0:
+                nc.scalar.copy(result[:], y_acc[n][:])
+            else:
+                nc.vector.tensor_copy(result[:], y_acc[n][:])
+            nc.sync.dma_start(out_0[P * n : P * (n + 1), :], result[:])
+        planes(1, (nc.vector.tensor_copy, nc.scalar.copy))
+        store_planes(1)

@@ -1,6 +1,7 @@
 from contextlib import ExitStack
 
 import concourse.mybir as mybir
+from concourse.masks import make_identity
 
 K, T, S, H, T2, M, N = 1536, 2048, 512, 1024, 1024, 512, 768
 FLOPS = 2 * (2 * K * H * S + H * N * M)
@@ -39,10 +40,10 @@ def tile_list_membrane_cleaning_features_kernel(
             return psum.tile([P, 512], F32, name="bank%d" % i, tag="bank%d" % i)
 
         def stage_tile():
-            return ring.tile([P, 2048], BF16, name="stage", tag="raw", bufs=4, align_bytes=64)
+            return ring.tile([P, 2048], BF16, name="stage", tag="raw", bufs=4, align_bytes=256)
 
         def held_tile(a, dtype, width):
-            return ring.tile([P, width], dtype, name="held", tag="held%d" % a, bufs=1, align_bytes=64)
+            return ring.tile([P, width], dtype, name="held", tag="held%d" % a, bufs=1, align_bytes=256)
 
         def quantize(codes, scales, staged):
             nc.vector.quantize_mx(out=codes.bitcast(FP8X4), scales=scales, in_=staged)
@@ -53,15 +54,11 @@ def tile_list_membrane_cleaning_features_kernel(
                 rows.rearrange("p t (c i) -> p c t i", i=4),
             )
 
-        tab_sc = first.tile([P, PASSES, T], U8, name="tab_sc", tag="bytes", bufs=2, align_bytes=64)
-        w2_sc_raw = first.tile([P, PASSES, H], U8, name="w2_sc_raw", align_bytes=64)
+        tab_sc = first.tile([P, PASSES, T], U8, name="tab_sc", tag="bytes0", bufs=1, align_bytes=256)
+        w2_sc_raw = first.tile([P, PASSES, H], U8, name="w2_sc_raw", tag="small", bufs=1, align_bytes=256)
         nc.vector.memset(tab_sc[:, 0:2, :].bitcast(I32), 0)
         nc.gpsimd.memset(tab_sc[:, 2, :].bitcast(I32), 0)
-        with tc.tile_pool(name="zero", bufs=1) as zero_pool:
-            zeros = zero_pool.tile([P, H // 4], I32, name="zeros")
-            nc.vector.memset(zeros[:], 0)
-            for a in range(PASSES):
-                nc.vector.tensor_copy(w2_sc_raw[:, a, :].bitcast(I32), zeros[:])
+        nc.vector.memset(w2_sc_raw[:].bitcast(I32), 0)
         keep = ctx.enter_context(tc.tile_pool(name="keep", bufs=1))
         ring = keep
 
@@ -69,41 +66,41 @@ def tile_list_membrane_cleaning_features_kernel(
         idx2 = lists.tile([P, S // 16], U16, name="idx2")
         idx3 = lists.tile([P, M // 16], U16, name="idx3")
         nc.sync.dma_start(idx1[:], offs)
-        nc.sync.dma_start(idx2[:], offs2)
-        nc.sync.dma_start(idx3[:], offs3)
-        w2_raw = first.tile([P, PASSES, 2 * H], U8, name="w2_raw", tag="bytes", bufs=2, align_bytes=64)
+        w2_raw = first.tile([P, PASSES, 2 * H], U8, name="w2_raw", tag="bytes1", bufs=1, align_bytes=256)
         nc.sync.dma_start(w2_raw[:].bitcast(I32), w2_words.rearrange("a p c -> p a c").bitcast(I32))
 
-        def load_scale_rows(tile, dram, q):
-            nc.sync.dma_start(
-                tile[32 * q : 32 * q + 4, :, :].bitcast(I32),
-                dram[:, 4 * q : 4 * q + 4, :].rearrange("a r c -> r a c").bitcast(I32),
+        def load_scale_rows(queue, tile, dram, r):
+            queue.dma_start(
+                tile[r:P:32, :, :].bitcast(I32),
+                dram.rearrange("a (q r) c -> r q a c", r=4)[r].bitcast(I32),
             )
 
         tab_w = []
 
         def load_table(a):
-            words = ring.tile([P, T], U32, name="tab_w", tag="early", bufs=3, align_bytes=64)
+            words = ring.tile([P, T], U32, name="tab_w", tag="early%d" % a, bufs=1, align_bytes=256)
             nc.sync.dma_start(words[:].bitcast(I32), tab_words[a].rearrange("p t i -> p (t i)").bitcast(I32))
             tab_w.append(words)
 
         for q in range(QUADS):
-            load_scale_rows(tab_sc, tab_scales, q)
+            load_scale_rows(nc.sync, tab_sc, tab_scales, q)
+        wgs_rows = ring.tile([P, S], F32, name="wgs_rows", tag="weighted", bufs=3, align_bytes=256)
+        nc.sync.dma_start(wgs_rows[:], wgs)
         load_table(0)
         for q in (0, 1):
-            load_scale_rows(w2_sc_raw, w2_scales, q)
+            load_scale_rows(nc.sync, w2_sc_raw, w2_scales, q)
         load_table(1)
         for q in (2, 3):
-            load_scale_rows(w2_sc_raw, w2_scales, q)
+            load_scale_rows(nc.sync, w2_sc_raw, w2_scales, q)
         load_table(2)
 
         w1_raw = {}
 
         def load_w1(g, a):
             if g == 0 and a < 2:
-                raw = ring.tile([P, PACK, KP], F32, name="w1_raw", tag="group%d" % a, bufs=1)
+                raw = ring.tile([P, PACK, KP], F32, name="w1_raw", tag="group%d" % a, bufs=1, align_bytes=256)
             else:
-                raw = ring.tile([P, PACK, KP], F32, name="w1_raw", tag="raw", bufs=4, align_bytes=64)
+                raw = ring.tile([P, PACK, KP], F32, name="w1_raw", tag="raw", bufs=4, align_bytes=256)
             nc.sync.dma_start(
                 raw[:], w1[KP * a : KP * (a + 1), KP * g : KP * (g + 1)].rearrange("(p j) c -> p j c", j=PACK)
             )
@@ -113,41 +110,66 @@ def tile_list_membrane_cleaning_features_kernel(
             return dram[KP * g : KP * (g + 1), :].rearrange("(p t) c -> t p c", t=PACK)[t]
 
         def load_page(g, t):
-            tile = keep.tile([P, T2], F32, name="page%d%d" % (g, t))
+            tile = keep.tile([P, T2], F32, name="page%d%d" % (g, t), align_bytes=256)
             nc.sync.dma_start(tile[:], dealt_rows(page0, g, t))
             return tile
 
         for a in range(PASSES):
             load_w1(0, a)
-        wg = keep.tile([P, PACK, S], F32, name="wg")
-        for q in (0, 2, 1, 3):
-            nc.sync.dma_start(wg[32 * q : 32 * (q + 1), :, :], wgs.rearrange("(p t) j -> p t j", t=PACK))
+        nc.sync.dma_start(idx2[:], offs2)
         page = {(0, 0): load_page(0, 0)}
+        nc.sync.dma_start(idx3[:], offs3)
         for a in range(PASSES):
             page[0, a + 1] = load_page(0, a + 1)
             load_w1(1, a)
-        gin_t = keep.tile([P, GROUPS, PACK], F32, name="gin_t")
-        gain_t = keep.tile([P, GROUPS, PACK], F32, name="gain_t")
+        gin_t = first.tile([P, GROUPS, PACK], F32, name="gin_t")
+        gain_t = first.tile([P, GROUPS, PACK], F32, name="gain_t")
         nc.sync.dma_start(gin_t[:], gin.rearrange("(g p t) -> p g t", g=GROUPS, t=PACK))
         nc.sync.dma_start(gain_t[:], gain.rearrange("(g p t) -> p g t", g=GROUPS, t=PACK))
         for t in range(PACK):
             page[1, t] = load_page(1, t)
         w3_raw = []
 
-        def load_w3():
-            for g in range(GROUPS):
-                raw = ring.tile([P, PACK, 512], F32, name="w3_raw", tag="early", bufs=3, align_bytes=64)
-                nc.sync.dma_start(raw[:], w3[KP * g : KP * (g + 1), 0:512].rearrange("(p j) c -> p j c", j=PACK))
-                w3_raw.append(raw)
-            rest = ring.tile([P, GROUPS, PACK, N - 512], F32, name="w3_rest", tag="early", bufs=3, align_bytes=64)
-            for g in range(GROUPS):
-                nc.sync.dma_start(
-                    rest[:, g, :, :], w3[KP * g : KP * (g + 1), 512:N].rearrange("(p j) c -> p j c", j=PACK)
-                )
-            w3_raw.append(rest)
+        def load_w3(piece):
+            raw = ring.tile([P, 2048], F32, name="w3_raw", tag="early%d" % piece, bufs=1, align_bytes=256)
+            if piece < GROUPS:
+                rows = w3[KP * piece : KP * (piece + 1), 0:512].rearrange("(p j) c -> p j c", j=PACK)
+                view = raw[:].rearrange("p (j c) -> p j c", j=PACK)
+                nc.sync.dma_start(view, rows)
+            else:
+                view = raw[:].rearrange("p (g j c) -> p g j c", g=GROUPS, j=PACK)
+                for g in range(GROUPS):
+                    rows = w3[KP * g : KP * (g + 1), 512:N].rearrange("(p j) c -> p j c", j=PACK)
+                    nc.sync.dma_start(view[:, g, :, :], rows)
+            w3_raw.append(view)
 
-        w2_c = [keep.tile([P, PASSES, 2 * KP], U8, name="w2_c%d" % g, align_bytes=64) for g in range(GROUPS)]
-        w2_s = [keep.tile([P, PASSES, KP], U8, name="w2_s%d" % g, align_bytes=64) for g in range(GROUPS)]
+        identity = ring.tile([P, P], F32, name="identity", tag="act", bufs=2)
+        make_identity(nc, identity[:])
+        turned = bank(4)
+        for c in range(PACK):
+            nc.tensor.transpose(turned[:, P * c : P * (c + 1)], wgs_rows[:, P * c : P * (c + 1)], identity[:])
+        spread = []
+        for c in range(PACK):
+            tile = ring.tile([P, S], F32, name="spread", tag="cells", bufs=4)
+            nc.scalar.copy(
+                tile[:].rearrange("j (t q p) -> j t q p", t=PACK, q=QUADS),
+                turned[:, P * c : P * (c + 1)]
+                .rearrange("j (p t) -> j t p", t=PACK)
+                .unsqueeze(2)
+                .broadcast_to([P, PACK, QUADS, 32]),
+            )
+            spread.append(tile)
+        wg = []
+        for t in range(PACK):
+            back = bank(t)
+            for c in range(PACK):
+                nc.tensor.transpose(back[:, P * c : P * (c + 1)], spread[c][:, P * t : P * (t + 1)], identity[:])
+            tile = keep.tile([P, S], F32, name="wg%d" % t)
+            nc.scalar.copy(tile[:], back[:])
+            wg.append(tile[:])
+
+        w2_c = [keep.tile([P, PASSES, 2 * KP], U8, name="w2_c%d" % g, align_bytes=256) for g in range(GROUPS)]
+        w2_s = [keep.tile([P, PASSES, KP], U8, name="w2_s%d" % g, align_bytes=256) for g in range(GROUPS)]
 
         def deal_w2_words(g):
             nc.vector.tensor_copy(
@@ -164,19 +186,19 @@ def tile_list_membrane_cleaning_features_kernel(
         deal_w2_words(0)
         v_w, v_planes = [], []
         for a in range(PASSES):
-            plane = keep.tile([P, S], U8, name="v_s%d" % a, align_bytes=64)
+            plane = keep.tile([P, S], U8, name="v_s%d" % a, align_bytes=256)
             nc.vector.tensor_copy(plane[:], tab_sc[:, a, :].indirect(idx1[:]))
             v_planes.append(plane)
         deal_w2_scales(0)
         for a in range(PASSES):
-            picked = keep.tile([P, S], U32, name="v_w%d" % a, align_bytes=64)
+            picked = keep.tile([P, S], U32, name="v_w%d" % a, align_bytes=256)
             nc.vector.tensor_copy(picked[:], tab_w[a][:].indirect(idx1[:]))
             v_w.append(picked)
 
         damp = {}
 
         def damping(g, t):
-            acc = bank(4 + t)
+            acc = bank(PACK * (1 - g) + t)
             for a in range(PASSES):
                 nc.tensor.matmul_mx(
                     out=acc[:],
@@ -189,12 +211,10 @@ def tile_list_membrane_cleaning_features_kernel(
                 )
             if g == 0 and t > 0:
                 size = held_tile(t - 1, F32, S)
-            elif g == 0:
-                size = ring.tile([P, S], F32, name="size", tag="group0", bufs=1)
             else:
                 size = ring.tile([P, S], F32, name="size", tag="act", bufs=2)
             nc.scalar.activation(size[:], acc[:], ACT.Abs)
-            root = ring.tile([P, S], F32, name="root", tag="damp", bufs=8)
+            root = ring.tile([P, S], F32, name="root", tag="damp", bufs=8, align_bytes=256)
             nc.scalar.activation(root[:], size[:], ACT.Abs_reciprocal_sqrt, bias=1.0)
             nc.scalar.activation(root[:], root[:], ACT.Square)
             damp[g, t] = root
@@ -204,11 +224,11 @@ def tile_list_membrane_cleaning_features_kernel(
         def quantize_w1(g, a, copy):
             staged = held_tile(a, BF16, 2048)
             copy(
-                staged[:].rearrange("p (t m j) -> p m j t", t=PACK, j=PACK),
-                w1_raw[g, a][:].rearrange("p j (m t) -> p m j t", t=PACK),
+                staged[:].rearrange("p (t m j) -> p m t j", t=PACK, j=PACK),
+                w1_raw[g, a][:].rearrange("p j (m t) -> p m t j", t=PACK),
             )
-            w1_c[g, a] = keep.tile([P, KP], U32, name="w1_c%d%d" % (g, a), align_bytes=64)
-            w1_s[g, a] = keep.tile([P, KP], U8, name="w1_s%d%d" % (g, a), align_bytes=64)
+            w1_c[g, a] = keep.tile([P, KP], U32, name="w1_c%d%d" % (g, a), align_bytes=256)
+            w1_s[g, a] = keep.tile([P, KP], U8, name="w1_s%d%d" % (g, a), align_bytes=256)
             quantize(w1_c[g, a][:], w1_s[g, a][:], staged[:])
 
         def first_products(g, first_bank):
@@ -226,31 +246,33 @@ def tile_list_membrane_cleaning_features_kernel(
                     )
             return accs
 
-        x_rows = {}
+        x_rows, late = {}, {}
 
         def renew(g, t, acc):
-            weighted = ring.tile([P, S], F32, name="weighted", tag="weighted", bufs=3)
-            nc.vector.tensor_tensor(weighted[:], acc[:], wg[:, t, :], MULT)
+            weighted = ring.tile([P, S], F32, name="weighted", tag="weighted", bufs=3, align_bytes=256)
+            nc.vector.tensor_tensor(weighted[:], acc[:], wg[t], MULT)
             nc.vector.tensor_tensor(page[g, t][:].indirect(idx2[:]), weighted[:], damp[g, t][:], MULT)
 
         def features(g, t):
             cells = ring.tile([P, M], F32, name="cells", tag="cells", bufs=4)
             nc.vector.tensor_copy(cells[:], page[g, t][:].indirect(idx3[:]))
             if g == 0:
-                bent = ring.tile([P, M], F32, name="bent", tag="act", bufs=2)
+                bent = ring.tile([P, M], F32, name="bent", tag="act", bufs=2)[:]
             else:
-                bent = ring.tile([P, M], F32, name="bent", tag="early", bufs=3, align_bytes=64)
-            nc.scalar.activation(bent[:], cells[:], ACT.Tanh, scale=gin_t[:, g, t : t + 1])
+                if t == 0:
+                    late["bent"] = ring.tile([P, PACK, M], F32, name="bent", tag="early2", bufs=1, align_bytes=256)
+                bent = late["bent"][:, t, :]
+            nc.scalar.activation(bent, cells[:], ACT.Tanh, scale=gin_t[:, g, t : t + 1])
             if t == 0:
-                x_rows[g] = first.tile([P, PACK, M], BF16, name="x_rows", tag="bytes", bufs=2, align_bytes=64)
-            nc.scalar.activation(x_rows[g][:, t, :], bent[:], ACT.Copy, scale=gain_t[:, g, t : t + 1])
+                x_rows[g] = first.tile([P, PACK, M], BF16, name="x_rows", tag="bytes%d" % g, bufs=1, align_bytes=256)
+            nc.scalar.activation(x_rows[g][:, t, :], bent, ACT.Copy, scale=gain_t[:, g, t : t + 1])
 
         grouped = {}
 
         def regroup(g, t):
             for h in range(2):
                 if t == 0:
-                    grouped[g, h] = ring.tile([P, PACK, HALF], F32, name="grouped", tag="group%d" % h, bufs=1)
+                    grouped[g, h] = ring.tile([P, PACK, HALF], F32, name="grouped", tag="group%d" % h, bufs=1, align_bytes=256)
                 nc.sync.dma_start(grouped[g, h][:, t, :], page[g, t][:, HALF * h : HALF * (h + 1)])
 
         def store_page(g):
@@ -258,31 +280,46 @@ def tile_list_membrane_cleaning_features_kernel(
                 rows = out_1[KP * g : KP * (g + 1), HALF * h : HALF * (h + 1)]
                 nc.sync.dma_start(rows.rearrange("(p t) c -> p t c", t=PACK), grouped[g, h][:])
 
-        page_c, page_s = {}, {}
+        page_c = {}
+        page_s = keep.tile([P, T2], U8, name="page_s", align_bytes=256)
 
-        def planes(g, copies):
-            page_c[g] = keep.tile([P, T2], U32, name="page_c%d" % g, align_bytes=64)
-            page_s[g] = keep.tile([P, T2], U8, name="page_s%d" % g, align_bytes=64)
+        page_staged = {}
+
+        def round_page(g, copies):
+            for h in range(2):
+                if g == 0:
+                    page_staged[g, h] = stage_tile()
+                elif h == 0:
+                    page_staged[g, h] = keep.tile([P, 2048], BF16, name="staged", tag="last0", bufs=1, align_bytes=256)
+                else:
+                    page_staged[g, h] = ring.tile([P, 2048], BF16, name="staged", tag="early2", bufs=1, align_bytes=256)
+                interleave(copies[h], page_staged[g, h][:], grouped[g, h][:])
+
+        def quantize_page(g):
+            if g == 0:
+                page_c[g] = first.tile([P, T2], U32, name="page_c0", tag="bytes1", bufs=1, align_bytes=256)
+            else:
+                page_c[g] = keep.tile([P, T2], U32, name="page_c1", align_bytes=256)
             for h in range(2):
                 cols = slice(HALF * h, HALF * (h + 1))
-                staged = stage_tile()
-                interleave(copies[h], staged[:], grouped[g, h][:])
-                quantize(page_c[g][:, cols], page_s[g][:, cols], staged[:])
+                quantize(page_c[g][:, cols], page_s[4 * g : P, cols], page_staged[g, h][:])
 
         def store_planes(g):
             nc.sync.dma_start(out_2[g].rearrange("p m t -> p (m t)").bitcast(I32), page_c[g][:].bitcast(I32))
-            for q in range(QUADS):
-                nc.sync.dma_start(
-                    out_3[g, 4 * q : 4 * q + 4, :].bitcast(I32), page_s[g][32 * q : 32 * q + 4, :].bitcast(I32)
-                )
 
         x_c, x_s = {}, {}
 
         def quantize_x(g, copy):
-            staged = stage_tile()
+            if g == 0:
+                staged = stage_tile()
+            else:
+                staged = keep.tile([P, 2048], BF16, name="x_staged", tag="last0", bufs=1, align_bytes=256)
             interleave(copy, staged[:], x_rows[g][:])
-            x_c[g] = keep.tile([P, M], U32, name="x_c%d" % g, align_bytes=64)
-            x_s[g] = keep.tile([P, M], U8, name="x_s%d" % g, align_bytes=64)
+            if g == 0:
+                x_c[g] = first.tile([P, M], U32, name="x_c0", tag="small", bufs=1, align_bytes=256)
+            else:
+                x_c[g] = keep.tile([P, M], U32, name="x_c1", align_bytes=256)
+            x_s[g] = keep.tile([P, M], U8, name="x_s%d" % g, align_bytes=256)
             quantize(x_c[g][:], x_s[g][:], staged[:])
 
         w3_c, w3_s = {}, {}
@@ -290,9 +327,9 @@ def tile_list_membrane_cleaning_features_kernel(
         def quantize_w3():
             for g in range(GROUPS):
                 staged = held_tile(g, BF16, 2048)
-                interleave(nc.scalar.copy, staged[:], w3_raw[g][:])
-                codes = keep.tile([P, 512], U32, name="w3_c%d" % g, align_bytes=64)
-                scales = keep.tile([P, 512], U8, name="w3_s%d" % g, align_bytes=64)
+                interleave(nc.scalar.copy, staged[:], w3_raw[g])
+                codes = keep.tile([P, 512], U32, name="w3_c%d" % g, align_bytes=256)
+                scales = keep.tile([P, 512], U8, name="w3_s%d" % g, align_bytes=256)
                 quantize(codes[:], scales[:], staged[:])
                 for n in range(4):
                     w3_c[g, n] = codes[:, P * n : P * (n + 1)]
@@ -300,8 +337,8 @@ def tile_list_membrane_cleaning_features_kernel(
             staged = held_tile(2, BF16, 2048)
             for g in range(GROUPS):
                 interleave(nc.scalar.copy, staged[:, 1024 * g : 1024 * (g + 1)], w3_raw[2][:, g, :, :])
-            codes = keep.tile([P, 512], U32, name="w3_c2", align_bytes=64)
-            scales = keep.tile([P, 512], U8, name="w3_s2", align_bytes=64)
+            codes = keep.tile([P, 512], U32, name="w3_c2", align_bytes=256)
+            scales = keep.tile([P, 512], U8, name="w3_s2", align_bytes=256)
             quantize(codes[:], scales[:], staged[:])
             for g in range(GROUPS):
                 for n in range(4, N // P):
@@ -320,9 +357,8 @@ def tile_list_membrane_cleaning_features_kernel(
                 stop=(g == GROUPS - 1),
             )
 
-        quantize_w1(0, 0, nc.scalar.copy)
         damping(0, 0)
-        for a in range(1, PASSES):
+        for a in range(PASSES):
             quantize_w1(0, a, nc.vector.tensor_copy)
         accs = first_products(0, 0)
         for t in range(1, PACK):
@@ -335,33 +371,38 @@ def tile_list_membrane_cleaning_features_kernel(
             quantize_w1(1, a, nc.scalar.copy)
         for t in range(PACK):
             damping(1, t)
-        accs = first_products(1, 0)
+        accs = first_products(1, 4)
         for t in range(PACK):
             features(0, t)
+            if t == PACK - 1:
+                load_w3(0)
             regroup(0, t)
-        load_w3()
+        load_w3(1)
+        load_w3(2)
         store_page(0)
         for t in range(PACK):
             renew(1, t, accs[t])
-        planes(0, (nc.scalar.copy, nc.scalar.copy))
+        round_page(0, (nc.scalar.copy, nc.scalar.copy))
         quantize_x(0, nc.scalar.copy)
         quantize_w3()
         for t in range(PACK):
             features(1, t)
             regroup(1, t)
         store_page(1)
-        store_planes(0)
-        y_acc = [bank((n + 4) % 8) for n in range(N // P)]
+        y_acc = [bank(n) for n in range(N // P)]
         for n in range(N // P):
             last_pass(0, n, y_acc[n])
         quantize_x(1, nc.vector.tensor_copy)
+        round_page(1, (nc.vector.tensor_copy, nc.scalar.copy))
         for n in range(N // P):
             last_pass(1, n, y_acc[n])
-            result = ring.tile([P, M], F32, name="result", tag="damp", bufs=8)
-            if n % 2 == 0:
-                nc.scalar.copy(result[:], y_acc[n][:])
-            else:
-                nc.vector.tensor_copy(result[:], y_acc[n][:])
+            result = ring.tile([P, M], F32, name="result", tag="damp", bufs=8, align_bytes=256)
+            nc.scalar.copy(result[:], y_acc[n][:])
             nc.sync.dma_start(out_0[P * n : P * (n + 1), :], result[:])
-        planes(1, (nc.vector.tensor_copy, nc.scalar.copy))
-        store_planes(1)
+        for g in range(GROUPS):
+            quantize_page(g)
+            store_planes(g)
+        for q in range(QUADS):
+            nc.sync.dma_start(
+                out_3[:, 4 * q : 4 * q + 4, :].bitcast(I32), page_s[32 * q : 32 * q + 4 * GROUPS, :].bitcast(I32)
+            )

@@ -254,7 +254,10 @@ def tile_list_membrane_cleaning_features_kernel(
             nc.vector.tensor_tensor(page[g, t][:].indirect(idx2[:]), weighted[:], damp[g, t][:], MULT)
 
         def features(g, t):
-            cells = ring.tile([P, M], F32, name="cells", tag="cells", bufs=4)
+            if g == 0 and t >= 2:
+                cells = held_tile(t - 1, F32, M)
+            else:
+                cells = ring.tile([P, M], F32, name="cells", tag="cells", bufs=4)
             nc.vector.tensor_copy(cells[:], page[g, t][:].indirect(idx3[:]))
             if g == 0:
                 bent = ring.tile([P, M], F32, name="bent", tag="act", bufs=2)[:]

from contextlib import ExitStack

import concourse.mybir as mybir
from concourse.masks import make_identity

K, T, S, H, T2, M, N = 1536, 2048, 512, 1024, 1024, 512, 768
FLOPS = 2 * (2 * K * H * S + H * N * M)

F32 = mybir.dt.float32
BF16 = mybir.dt.bfloat16
I32 = mybir.dt.int32
U32 = mybir.dt.uint32
U16 = mybir.dt.uint16
U8 = mybir.dt.uint8
FP8X4 = mybir.dt.float8_e4m3fn_x4
FP4X4 = mybir.dt.float4_e2m1fn_x4
ACT = mybir.ActivationFunctionType
MULT = mybir.AluOpType.mult

P = 128
PACK = 4
KP = P * PACK
PASSES = K // KP
GROUPS = H // KP
QUADS = 4
HALF = T2 // 2


def tile_list_membrane_cleaning_features_kernel(
    tc, tab_words, tab_scales, offs, offs2, offs3, w1, w2_words, w2_scales, wgs, page0, gin, gain, w3,
    out_0, out_1, out_2, out_3,
):
    nc = tc.nc
    with ExitStack() as ctx:
        lists = ctx.enter_context(tc.tile_pool(name="lists", bufs=1))
        first = ctx.enter_context(tc.tile_pool(name="first", bufs=1))
        psum = ctx.enter_context(tc.psum_pool(name="psum", bufs=1))

        def bank(i):
            return psum.tile([P, 512], F32, name="bank%d" % i, tag="bank%d" % i)

        def stage_tile():
            return ring.tile([P, 2048], BF16, name="stage", tag="raw", bufs=4, align_bytes=256)

        def held_tile(a, dtype, width):
            return ring.tile([P, width], dtype, name="held", tag="held%d" % a, bufs=1, align_bytes=256)

        def quantize(codes, scales, staged):
            nc.vector.quantize_mx(out=codes.bitcast(FP8X4), scales=scales, in_=staged)

        def interleave(copy, staged, rows):
            copy(
                staged.rearrange("p (c i t) -> p c t i", i=4, t=PACK),
                rows.rearrange("p t (c i) -> p c t i", i=4),
            )

        tab_sc = first.tile([P, PASSES, T], U8, name="tab_sc", tag="bytes0", bufs=1, align_bytes=256)
        w2_sc_raw = first.tile([P, PASSES, H], U8, name="w2_sc_raw", tag="small", bufs=1, align_bytes=256)
        nc.vector.memset(tab_sc[:, 0:2, :].bitcast(I32), 0)
        nc.gpsimd.memset(tab_sc[:, 2, :].bitcast(I32), 0)
        nc.vector.memset(w2_sc_raw[:].bitcast(I32), 0)
        keep = ctx.enter_context(tc.tile_pool(name="keep", bufs=1))
        ring = keep

        idx1 = lists.tile([P, S // 16], U16, name="idx1")
        idx2 = lists.tile([P, S // 16], U16, name="idx2")
        idx3 = lists.tile([P, M // 16], U16, name="idx3")
        nc.sync.dma_start(idx1[:], offs)
        w2_raw = first.tile([P, PASSES, 2 * H], U8, name="w2_raw", tag="bytes1", bufs=1, align_bytes=256)
        nc.sync.dma_start(w2_raw[:].bitcast(I32), w2_words.rearrange("a p c -> p a c").bitcast(I32))

        def load_scale_rows(queue, tile, dram, r):
            queue.dma_start(
                tile[r:P:32, :, :].bitcast(I32),
                dram.rearrange("a (q r) c -> r q a c", r=4)[r].bitcast(I32),
            )

        tab_w = []

        def load_table(a):
            words = ring.tile([P, T], U32, name="tab_w", tag="early%d" % a, bufs=1, align_bytes=256)
            nc.sync.dma_start(words[:].bitcast(I32), tab_words[a].rearrange("p t i -> p (t i)").bitcast(I32))
            tab_w.append(words)

        for q in range(QUADS):
            load_scale_rows(nc.sync, tab_sc, tab_scales, q)
        wgs_rows = ring.tile([P, S], F32, name="wgs_rows", tag="weighted", bufs=3, align_bytes=256)
        nc.sync.dma_start(wgs_rows[:], wgs)
        load_table(0)
        for q in (0, 1):
            load_scale_rows(nc.sync, w2_sc_raw, w2_scales, q)
        load_table(1)
        for q in (2, 3):
            load_scale_rows(nc.sync, w2_sc_raw, w2_scales, q)
        load_table(2)

        w1_raw = {}

        def load_w1(g, a):
            if g == 0 and a < 2:
                raw = ring.tile([P, PACK, KP], F32, name="w1_raw", tag="group%d" % a, bufs=1, align_bytes=256)
            else:
                raw = ring.tile([P, PACK, KP], F32, name="w1_raw", tag="raw", bufs=4, align_bytes=256)
            nc.sync.dma_start(
                raw[:], w1[KP * a : KP * (a + 1), KP * g : KP * (g + 1)].rearrange("(p j) c -> p j c", j=PACK)
            )
            w1_raw[g, a] = raw

        def dealt_rows(dram, g, t):
            return dram[KP * g : KP * (g + 1), :].rearrange("(p t) c -> t p c", t=PACK)[t]

        def load_page(g, t):
            tile = keep.tile([P, T2], F32, name="page%d%d" % (g, t), align_bytes=256)
            nc.sync.dma_start(tile[:], dealt_rows(page0, g, t))
            return tile

        for a in range(PASSES):
            load_w1(0, a)
        nc.sync.dma_start(idx2[:], offs2)
        page = {(0, 0): load_page(0, 0)}
        nc.sync.dma_start(idx3[:], offs3)
        for a in range(PASSES):
            page[0, a + 1] = load_page(0, a + 1)
            load_w1(1, a)
        gin_t = first.tile([P, GROUPS, PACK], F32, name="gin_t")
        gain_t = first.tile([P, GROUPS, PACK], F32, name="gain_t")
        nc.sync.dma_start(gin_t[:], gin.rearrange("(g p t) -> p g t", g=GROUPS, t=PACK))
        nc.sync.dma_start(gain_t[:], gain.rearrange("(g p t) -> p g t", g=GROUPS, t=PACK))
        for t in range(PACK):
            page[1, t] = load_page(1, t)
        w3_raw = []

        def load_w3(piece):
            raw = ring.tile([P, 2048], F32, name="w3_raw", tag="early%d" % piece, bufs=1, align_bytes=256)
            if piece < GROUPS:
                rows = w3[KP * piece : KP * (piece + 1), 0:512].rearrange("(p j) c -> p j c", j=PACK)
                view = raw[:].rearrange("p (j c) -> p j c", j=PACK)
                nc.sync.dma_start(view, rows)
            else:
                view = raw[:].rearrange("p (g j c) -> p g j c", g=GROUPS, j=PACK)
                for g in range(GROUPS):
                    rows = w3[KP * g : KP * (g + 1), 512:N].rearrange("(p j) c -> p j c", j=PACK)
                    nc.sync.dma_start(view[:, g, :, :], rows)
            w3_raw.append(view)

        identity = ring.tile([P, P], F32, name="identity", tag="act", bufs=2)
        make_identity(nc, identity[:])
        turned = bank(4)
        for c in range(PACK):
            nc.tensor.transpose(turned[:, P * c : P * (c + 1)], wgs_rows[:, P * c : P * (c + 1)], identity[:])
        spread = []
        for c in range(PACK):
            tile = ring.tile([P, S], F32, name="spread", tag="cells", bufs=4)
            nc.scalar.copy(
                tile[:].rearrange("j (t q p) -> j t q p", t=PACK, q=QUADS),
                turned[:, P * c : P * (c + 1)]
                .rearrange("j (p t) -> j t p", t=PACK)
                .unsqueeze(2)
                .broadcast_to([P, PACK, QUADS, 32]),
            )
            spread.append(tile)
        wg = []
        for t in range(PACK):
            back = bank(t)
            for c in range(PACK):
                nc.tensor.transpose(back[:, P * c : P * (c + 1)], spread[c][:, P * t : P * (t + 1)], identity[:])
            tile = keep.tile([P, S], F32, name="wg%d" % t)
            nc.scalar.copy(tile[:], back[:])
            wg.append(tile[:])

        w2_c = [keep.tile([P, PASSES, 2 * KP], U8, name="w2_c%d" % g, align_bytes=256) for g in range(GROUPS)]
        w2_s = [keep.tile([P, PASSES, KP], U8, name="w2_s%d" % g, align_bytes=256) for g in range(GROUPS)]

        def deal_w2_words(g):
            nc.vector.tensor_copy(
                w2_c[g][:].bitcast(U16).rearrange("p a (t m) -> p t a m", t=PACK),
                w2_raw[:].bitcast(U16)[:, :, KP * g : KP * (g + 1)].rearrange("p a (m t) -> p t a m", t=PACK),
            )

        def deal_w2_scales(g):
            nc.vector.tensor_copy(
                w2_s[g][:].rearrange("p a (t m) -> p t a m", t=PACK),
                w2_sc_raw[:, :, KP * g : KP * (g + 1)].rearrange("p a (m t) -> p t a m", t=PACK),
            )

        deal_w2_words(0)
        v_w, v_planes = [], []
        for a in range(PASSES):
            plane = keep.tile([P, S], U8, name="v_s%d" % a, align_bytes=256)
            nc.vector.tensor_copy(plane[:], tab_sc[:, a, :].indirect(idx1[:]))
            v_planes.append(plane)
        deal_w2_scales(0)
        for a in range(PASSES):
            picked = keep.tile([P, S], U32, name="v_w%d" % a, align_bytes=256)
            nc.vector.tensor_copy(picked[:], tab_w[a][:].indirect(idx1[:]))
            v_w.append(picked)

        damp = {}

        def damping(g, t):
            acc = bank(PACK * (1 - g) + t)
            for a in range(PASSES):
                nc.tensor.matmul_mx(
                    out=acc[:],
                    lhsT=w2_c[g][:, a, 2 * P * t : 2 * P * (t + 1)].bitcast(FP4X4),
                    lhsT_scale=w2_s[g][:, a, P * t : P * (t + 1)],
                    rhs=v_w[a][:].bitcast(FP8X4),
                    rhs_scale=v_planes[a][:],
                    start=(a == 0),
                    stop=(a == PASSES - 1),
                )
            if g == 0 and t > 0:
                size = held_tile(t - 1, F32, S)
            else:
                size = ring.tile([P, S], F32, name="size", tag="act", bufs=2)
            nc.scalar.activation(size[:], acc[:], ACT.Abs)
            root = ring.tile([P, S], F32, name="root", tag="damp", bufs=8, align_bytes=256)
            nc.scalar.activation(root[:], size[:], ACT.Abs_reciprocal_sqrt, bias=1.0)
            nc.scalar.activation(root[:], root[:], ACT.Square)
            damp[g, t] = root

        w1_c, w1_s = {}, {}

        def quantize_w1(g, a, copy):
            staged = held_tile(a, BF16, 2048)
            copy(
                staged[:].rearrange("p (t m j) -> p m t j", t=PACK, j=PACK),
                w1_raw[g, a][:].rearrange("p j (m t) -> p m t j", t=PACK),
            )
            w1_c[g, a] = keep.tile([P, KP], U32, name="w1_c%d%d" % (g, a), align_bytes=256)
            w1_s[g, a] = keep.tile([P, KP], U8, name="w1_s%d%d" % (g, a), align_bytes=256)
            quantize(w1_c[g, a][:], w1_s[g, a][:], staged[:])

        def first_products(g, first_bank):
            accs = [bank(first_bank + t) for t in range(PACK)]
            for a in range(PASSES):
                for t in range(PACK):
                    nc.tensor.matmul_mx(
                        out=accs[t][:],
                        lhsT=w1_c[g, a][:, P * t : P * (t + 1)].bitcast(FP8X4),
                        lhsT_scale=w1_s[g, a][:, P * t : P * (t + 1)],
                        rhs=v_w[a][:].bitcast(FP8X4),
                        rhs_scale=v_planes[a][:],
                        start=(a == 0),
                        stop=(a == PASSES - 1),
                    )
            return accs

        x_rows, late = {}, {}

        def renew(g, t, acc):
            weighted = ring.tile([P, S], F32, name="weighted", tag="weighted", bufs=3, align_bytes=256)
            nc.vector.tensor_tensor(weighted[:], acc[:], wg[t], MULT)
            nc.vector.tensor_tensor(page[g, t][:].indirect(idx2[:]), weighted[:], damp[g, t][:], MULT)

        def features(g, t):
            if g == 0 and t >= 2:
                cells = held_tile(t - 1, F32, M)
            else:
                cells = ring.tile([P, M], F32, name="cells", tag="cells", bufs=4)
            nc.vector.tensor_copy(cells[:], page[g, t][:].indirect(idx3[:]))
            if g == 0:
                bent = ring.tile([P, M], F32, name="bent", tag="act", bufs=2)[:]
            else:
                if t == 0:
                    late["bent"] = ring.tile([P, PACK, M], F32, name="bent", tag="early2", bufs=1, align_bytes=256)
                bent = late["bent"][:, t, :]
            nc.scalar.activation(bent, cells[:], ACT.Tanh, scale=gin_t[:, g, t : t + 1])
            if t == 0:
                x_rows[g] = first.tile([P, PACK, M], BF16, name="x_rows", tag="bytes%d" % g, bufs=1, align_bytes=256)
            nc.scalar.activation(x_rows[g][:, t, :], bent, ACT.Copy, scale=gain_t[:, g, t : t + 1])

        grouped = {}

        def regroup(g, t):
            for h in range(2):
                if t == 0:
                    grouped[g, h] = ring.tile([P, PACK, HALF], F32, name="grouped", tag="group%d" % h, bufs=1, align_bytes=256)
                nc.sync.dma_start(grouped[g, h][:, t, :], page[g, t][:, HALF * h : HALF * (h + 1)])

        def store_page(g):
            for h in range(2):
                rows = out_1[KP * g : KP * (g + 1), HALF * h : HALF * (h + 1)]
                nc.sync.dma_start(rows.rearrange("(p t) c -> p t c", t=PACK), grouped[g, h][:])

        page_c = {}
        page_s = keep.tile([P, T2], U8, name="page_s", align_bytes=256)

        page_staged = {}

        def round_page(g, copies):
            for h in range(2):
                if g == 0:
                    page_staged[g, h] = stage_tile()
                elif h == 0:
                    page_staged[g, h] = keep.tile([P, 2048], BF16, name="staged", tag="last0", bufs=1, align_bytes=256)
                else:
                    page_staged[g, h] = ring.tile([P, 2048], BF16, name="staged", tag="early2", bufs=1, align_bytes=256)
                interleave(copies[h], page_staged[g, h][:], grouped[g, h][:])

        def quantize_page(g):
            if g == 0:
                page_c[g] = first.tile([P, T2], U32, name="page_c0", tag="bytes1", bufs=1, align_bytes=256)
            else:
                page_c[g] = keep.tile([P, T2], U32, name="page_c1", align_bytes=256)
            for h in range(2):
                cols = slice(HALF * h, HALF * (h + 1))
                quantize(page_c[g][:, cols], page_s[4 * g : P, cols], page_staged[g, h][:])

        def store_planes(g):
            nc.sync.dma_start(out_2[g].rearrange("p m t -> p (m t)").bitcast(I32), page_c[g][:].bitcast(I32))

        x_c, x_s = {}, {}

        def quantize_x(g, copy):
            if g == 0:
                staged = stage_tile()
            else:
                staged = keep.tile([P, 2048], BF16, name="x_staged", tag="last0", bufs=1, align_bytes=256)
            interleave(copy, staged[:], x_rows[g][:])
            if g == 0:
                x_c[g] = first.tile([P, M], U32, name="x_c0", tag="small", bufs=1, align_bytes=256)
            else:
                x_c[g] = keep.tile([P, M], U32, name="x_c1", align_bytes=256)
            x_s[g] = keep.tile([P, M], U8, name="x_s%d" % g, align_bytes=256)
            quantize(x_c[g][:], x_s[g][:], staged[:])

        w3_c, w3_s = {}, {}

        def quantize_w3():
            for g in range(GROUPS):
                staged = held_tile(g, BF16, 2048)
                interleave(nc.scalar.copy, staged[:], w3_raw[g])
                codes = keep.tile([P, 512], U32, name="w3_c%d" % g, align_bytes=256)
                scales = keep.tile([P, 512], U8, name="w3_s%d" % g, align_bytes=256)
                quantize(codes[:], scales[:], staged[:])
                for n in range(4):
                    w3_c[g, n] = codes[:, P * n : P * (n + 1)]
                    w3_s[g, n] = scales[:, P * n : P * (n + 1)]
            staged = held_tile(2, BF16, 2048)
            for g in range(GROUPS):
                interleave(nc.scalar.copy, staged[:, 1024 * g : 1024 * (g + 1)], w3_raw[2][:, g, :, :])
            codes = keep.tile([P, 512], U32, name="w3_c2", align_bytes=256)
            scales = keep.tile([P, 512], U8, name="w3_s2", align_bytes=256)
            quantize(codes[:], scales[:], staged[:])
            for g in range(GROUPS):
                for n in range(4, N // P):
                    cols = slice(256 * g + P * (n - 4), 256 * g + P * (n - 3))
                    w3_c[g, n] = codes[:, cols]
                    w3_s[g, n] = scales[:, cols]

        def last_pass(g, n, acc):
            nc.tensor.matmul_mx(
                out=acc[:],
                lhsT=w3_c[g, n].bitcast(FP8X4),
                lhsT_scale=w3_s[g, n],
                rhs=x_c[g][:].bitcast(FP8X4),
                rhs_scale=x_s[g][:],
                start=(g == 0),
                stop=(g == GROUPS - 1),
            )

        damping(0, 0)
        for a in range(PASSES):
            quantize_w1(0, a, nc.vector.tensor_copy)
        accs = first_products(0, 0)
        for t in range(1, PACK):
            damping(0, t)
        deal_w2_words(1)
        deal_w2_scales(1)
        for t in range(PACK):
            renew(0, t, accs[t])
        for a in range(PASSES):
            quantize_w1(1, a, nc.scalar.copy)
        for t in range(PACK):
            damping(1, t)
        accs = first_products(1, 4)
        for t in range(PACK):
            features(0, t)
            if t == PACK - 1:
                load_w3(0)
            regroup(0, t)
        load_w3(1)
        load_w3(2)
        store_page(0)
        for t in range(PACK):
            renew(1, t, accs[t])
        round_page(0, (nc.scalar.copy, nc.scalar.copy))
        quantize_x(0, nc.scalar.copy)
        quantize_w3()
        for t in range(PACK):
            features(1, t)
            regroup(1, t)
        store_page(1)
        y_acc = [bank(n) for n in range(N // P)]
        for n in range(N // P):
            last_pass(0, n, y_acc[n])
        quantize_x(1, nc.vector.tensor_copy)
        round_page(1, (nc.vector.tensor_copy, nc.scalar.copy))
        for n in range(N // P):
            last_pass(1, n, y_acc[n])
            result = ring.tile([P, M], F32, name="result", tag="damp", bufs=8, align_bytes=256)
            nc.scalar.copy(result[:], y_acc[n][:])
            nc.sync.dma_start(out_0[P * n : P * (n + 1), :], result[:])
        for g in range(GROUPS):
            quantize_page(g)
            store_planes(g)
        for q in range(QUADS):
            nc.sync.dma_start(
                out_3[:, 4 * q : 4 * q + 4, :].bitcast(I32), page_s[32 * q : 32 * q + 4 * GROUPS, :].bitcast(I32)
            )
